import numpy as np
import ml_dtypes


def mxq(x, axis, fmt="e4m3"):
    dtype, down = {"e4m3": (ml_dtypes.float8_e4m3fn, 7), "e5m2": (ml_dtypes.float8_e5m2, 14)}[fmt]
    v = np.moveaxis(np.asarray(x, np.float32).astype(ml_dtypes.bfloat16).astype(np.float64), axis, -1)
    blocks = v.reshape(v.shape[:-1] + (-1, 32))
    amax = np.abs(blocks).max(-1, keepdims=True)
    byte = np.maximum(np.where(amax > 0, np.frexp(amax)[1] - 1 + 127, 0) - down, 1)
    scale = np.exp2(byte - 127.0)
    codes = (blocks / scale).astype(np.float32).astype(dtype).astype(np.float64)
    return np.moveaxis((codes * scale).reshape(v.shape), -1, axis)


WIDE = False


def mx_kscale(k):
    if not WIDE:
        return np.ones(k)
    levels = np.array([10, -10, 5, -5, 0])
    if k % 512:
        return np.exp2(np.random.permutation(np.resize(levels, k // 32))).repeat(32)
    a = np.empty((k // 512, 16))
    for p in range(k // 512):
        a[p, :8] = np.random.permutation(np.resize(levels, 8))
        for g in range(8):
            far = levels[np.abs(levels - a[p, g]) >= 10]
            a[p, g + 8] = far[np.random.randint(len(far))]
    return np.exp2(a.ravel()).repeat(32)


def f64(x):
    return np.asarray(x).astype(np.float64)


def striped(idx):
    return np.tile(np.asarray(idx).reshape(-1, 16).T, (8, 1)).astype(np.uint16)


def unstriped(offs):
    return offs[:16].T.reshape(-1).astype(np.int64)


def striped8(idx):
    return np.asarray(idx).reshape(8, -1, 16).transpose(0, 2, 1).reshape(128, -1).astype(np.uint16)


def unstriped8(offs):
    return offs.reshape(8, 16, -1).transpose(0, 2, 1).reshape(8, -1).astype(np.int64)


def pick8(x, idx, run):
    r = np.arange(len(x))
    return x[r[:, None], idx[r % (8 * run) // run]]


E2M1 = np.array([0.0, 0.5, 1.0, 1.5, 2.0, 3.0, 4.0, 6.0, -0.0, -0.5, -1.0, -1.5, -2.0, -3.0, -4.0, -6.0])


def pack_weight(w, fmt):
    k, n = w.shape
    w = f64(np.asarray(w, np.float32).astype(ml_dtypes.bfloat16)).reshape(k // 32, 32, n)
    amax = np.abs(w).max(1)
    if fmt == "e4m3":
        byte = np.frexp(amax)[1] - 1 + 127 - 7
    else:
        mant, ex = np.frexp(amax / 6.0)
        byte = np.where(mant > 0.5, ex, ex - 1) + 127
    byte = np.clip(np.where(amax > 0, byte, 1), 1, 254)
    scaled = (w * np.exp2(127.0 - byte)[:, None, :]).reshape(k, n).astype(np.float32)
    by_word = np.ascontiguousarray(scaled.reshape(k // 512, 128, 4, n).transpose(0, 1, 3, 2))
    if fmt == "e4m3":
        words = by_word.astype(ml_dtypes.float8_e4m3fn).view(np.uint8)
    else:
        c = by_word.astype(ml_dtypes.float4_e2m1fn).view(np.uint8) & 0xF
        words = (c[..., 0::2] | (c[..., 1::2] << 4)).reshape(k // 512, 128, 2 * n)
    return np.ascontiguousarray(words), np.ascontiguousarray(byte.astype(np.uint8).reshape(k // 512, 16, n))


def unpack_weight(words, scales, fmt):
    g, _, n = scales.shape
    words = np.ascontiguousarray(words).reshape(g, 128, n, -1)
    if fmt == "e4m3":
        vals = words.view(ml_dtypes.float8_e4m3fn).astype(np.float64)
    else:
        nib = np.empty((g, 128, n, 4), np.uint8)
        nib[..., 0::2] = words & 0xF
        nib[..., 1::2] = words >> 4
        vals = E2M1[nib]
    vals = vals * np.repeat(np.exp2(scales.astype(np.float64) - 127.0), 8, axis=1)[..., None]
    return vals.transpose(0, 1, 3, 2).reshape(g * 512, n)


def sigmoid(v):
    return 1.0 / (1.0 + np.exp(-v))


def sgn(shape):
    return np.random.uniform(0.5, 2.0, shape) * np.where(np.random.standard_normal(shape) < 0, -1.0, 1.0)


K, J, R, T, Z, M, C, O, N = 512, 256, 512, 1024, 512, 1024, 512, 256, 256


def setup_inputs():
    n = np.random.standard_normal
    idx = np.random.permutation(T)[:J]
    idx2 = np.random.permutation(M)[:J]
    idx3 = np.stack([np.random.permutation(C)[:J] for _ in range(8)])
    idx4 = np.stack([np.random.permutation(C)[:J] for _ in range(8)])
    idx5 = np.stack([np.random.permutation(C)[:O] for _ in range(8)])
    idx6 = np.stack([np.random.permutation(C)[:O] for _ in range(8)])
    fk = mx_kscale(K)
    fr = mx_kscale(R)
    fz = mx_kscale(Z)
    xtp = pack_weight(n((K, T)) * fk[:, None], "e4m3")
    wp = pack_weight(n((K, R)) * 1 / np.sqrt(K) / fk[:, None] * fr, "e2m1")
    xop = pack_weight(n((Z, M)) / fz[:, None], "e2m1")
    w2p = pack_weight(n((Z, R)) * 1 / np.sqrt(Z) * fz[:, None], "e4m3")
    wbp = pack_weight(n((R, N)) * 1 / np.sqrt(R) / fr[:, None], "e4m3")
    return {
        "xt_words": xtp[0],
        "xt_scales": xtp[1],
        "w_words": wp[0],
        "w_scales": wp[1],
        "xo_words": xop[0],
        "xo_scales": xop[1],
        "w2_words": w2p[0],
        "w2_scales": w2p[1],
        "sl": (sgn((R, 1))).astype(np.float32),
        "gf": (np.random.uniform(-1.0, 1.0, (R, 1))).astype(np.float32),
        "sa": (np.random.uniform(0.5, 1.6, (R, 1))).astype(np.float32),
        "wb_words": wbp[0],
        "wb_scales": wbp[1],
        "offs": striped(idx),
        "offs2": striped(idx2),
        "offs3": striped8(idx3),
        "offs4": striped8(idx4),
        "offs5": striped8(idx5),
        "offs6": striped8(idx6),
    }


def reference(xt_words, xt_scales, w_words, w_scales, xo_words, xo_scales, w2_words, w2_scales, sl, gf, sa, wb_words, wb_scales, offs, offs2, offs3, offs4, offs5, offs6):
    idx = unstriped(offs)
    idx2 = unstriped(offs2)
    idx3 = unstriped8(offs3)
    idx4 = unstriped8(offs4)
    idx5 = unstriped8(offs5)
    idx6 = unstriped8(offs6)
    xtu = unpack_weight(xt_words, xt_scales, "e4m3")
    wu = unpack_weight(w_words, w_scales, "e2m1")
    xou = unpack_weight(xo_words, xo_scales, "e2m1")
    w2u = unpack_weight(w2_words, w2_scales, "e4m3")
    wbu = unpack_weight(wb_words, wb_scales, "e4m3")
    xtidxg = xtu[:, idx]
    a = wu.T @ xtidxg
    xoidx2g = xou[:, idx2]
    b = w2u.T @ xoidx2g
    pw = np.zeros((R, C))
    pw[np.arange(R)[:, None], idx3[np.arange(R) % 512 // 64]] = a
    pv = np.zeros((R, C))
    pv[np.arange(R)[:, None], idx4[np.arange(R) % 512 // 64]] = b
    hid = pick8(pw, idx5, 64) * f64(sa) * sigmoid(pick8(pv, idx6, 64) * f64(sl) + f64(gf))
    hidq = mxq(hid, 0, "e4m3")
    y = wbu.T @ hidq
    return y

@@ -1,0 +1,190 @@
+from contextlib import ExitStack
+
+import concourse.mybir as mybir
+
+F32 = mybir.dt.float32
+BF16 = mybir.dt.bfloat16
+I32 = mybir.dt.int32
+U32 = mybir.dt.uint32
+U16 = mybir.dt.uint16
+U8 = mybir.dt.uint8
+FP8X4 = mybir.dt.float8_e4m3fn_x4
+FP4X4 = mybir.dt.float4_e2m1fn_x4
+ACT = mybir.ActivationFunctionType
+MULT = mybir.AluOpType.mult
+
+K, J, R, T, Z, M, C, O, N = 512, 256, 512, 1024, 512, 1024, 512, 256, 256
+P = 128
+PACK = 4
+QUADS = 4
+HALF = O // 2
+FLOPS = 2 * K * R * J + 2 * Z * R * J + 2 * R * N * O
+
+
+def tile_picked_tokens_gate_two_sigmoidboard_one_plain_kernel(
+    tc, xt_words, xt_scales, w_words, w_scales, xo_words, xo_scales, w2_words, w2_scales,
+    sl, gf, sa, wb_words, wb_scales, offs, offs2, offs3, offs4, offs5, offs6, out,
+):
+    nc = tc.nc
+    with ExitStack() as ctx:
+        keep = ctx.enter_context(tc.tile_pool(name="keep", bufs=1))
+        psum = ctx.enter_context(tc.psum_pool(name="psum", bufs=4))
+
+        def sb(name, shape, dtype):
+            return keep.tile(shape, dtype, name=name, align_bytes=64)
+
+        def load_list(name, src):
+            lst = sb(name, [P, J // 16], U16)
+            nc.sync.dma_start(lst[:], src)
+            return lst
+
+        def zeroed_plane(name, width):
+            plane = sb(name, [P, width], U8)
+            nc.vector.memset(plane[:].bitcast(I32), 0)
+            return plane
+
+        def load_plane(plane, scales):
+            for q in range(QUADS):
+                nc.sync.dma_start(plane[32 * q : 32 * q + 4, :].bitcast(I32), scales[0, 4 * q : 4 * q + 4, :].bitcast(I32))
+
+        def load_rows(name, src):
+            col = sb(name, [P, PACK], F32)
+            nc.sync.dma_start(col[:], src.rearrange("(p t) o -> p (t o)", t=PACK))
+            return col
+
+        xo_plane = zeroed_plane("xo_plane", M)
+        w2_plane = zeroed_plane("w2_plane", R)
+        xt_plane = zeroed_plane("xt_plane", T)
+        w_plane = zeroed_plane("w_plane", R)
+        wb_plane = zeroed_plane("wb_plane", N)
+        gate_boards = [sb("pv%d" % i, [P, C], F32) for i in range(2)]
+        value_boards = [sb("pw%d" % i, [P, C], F32) for i in range(2)]
+        for board in gate_boards + value_boards:
+            nc.vector.memset(board[:], 0.0)
+
+        xo_win = sb("xo_win", [P, M], U16)
+        nc.scalar.dma_start(xo_win[:].bitcast(I32), xo_words[0].bitcast(I32))
+        w2_raw = sb("w2_raw", [P, R], U32)
+        nc.scalar.dma_start(w2_raw[:].bitcast(I32), w2_words[0].rearrange("p n t -> p (n t)").bitcast(I32))
+        l2 = load_list("l2", offs2)
+        w2_stage = sb("w2_stage", [4, QUADS, R // 4], I32)
+        nc.sync.dma_start(w2_stage[:], w2_scales[0].bitcast(I32).rearrange("(q i) n -> i q n", i=4))
+        load_plane(xo_plane, xo_scales)
+        l4 = load_list("l4", offs4)
+        l1 = load_list("l1", offs)
+        load_plane(xt_plane, xt_scales)
+        xt_win = sb("xt_win", [P, T], U32)
+        nc.sync.dma_start(xt_win[:].bitcast(I32), xt_words[0].rearrange("p n t -> p (n t)").bitcast(I32))
+        w_raw = sb("w_raw", [P, 2 * R], U8)
+        nc.sync.dma_start(w_raw[:].bitcast(I32), w_words[0].bitcast(I32))
+        l6 = load_list("l6", offs6)
+        slope = load_rows("slope", sl)
+        offset = load_rows("offset", gf)
+        load_plane(w_plane, w_scales)
+        l3 = load_list("l3", offs3)
+        l5 = load_list("l5", offs5)
+        weight = load_rows("weight", sa)
+        wb_codes = sb("wb_codes", [P, N], U32)
+        nc.sync.dma_start(wb_codes[:].bitcast(I32), wb_words[0].rearrange("p n t -> p (n t)").bitcast(I32))
+        load_plane(wb_plane, wb_scales)
+
+        for q in range(QUADS):
+            nc.vector.tensor_copy(w2_plane[32 * q : 32 * q + 4, :].bitcast(I32), w2_stage[0:4, q, :])
+        xo_sc = sb("xo_sc", [P, J], U8)
+        nc.vector.tensor_copy(xo_sc[:], xo_plane[:].indirect(l2[:]))
+        xo_codes = sb("xo_codes", [P, J], U16)
+        nc.vector.tensor_copy(xo_codes[:], xo_win[:].indirect(l2[:]))
+
+        def product(name, codes, scales, rhs, rhs_scale):
+            acc = psum.tile([P, J], F32, name="acc")
+            nc.tensor.matmul_mx(out=acc[:], lhsT=codes, lhsT_scale=scales, rhs=rhs, rhs_scale=rhs_scale, start=True, stop=True)
+            res = sb(name, [P, J], F32)
+            nc.vector.tensor_copy(res[:], acc[:])
+            return res
+
+        b_res = []
+        for t in range(PACK):
+            codes = sb("w2c%d" % t, [P, P], U32)
+            scales = sb("w2s%d" % t, [P, P], U8)
+            nc.vector.tensor_copy(scales[:], w2_plane[:, t::PACK])
+            if t == 0:
+                nc.scalar.copy(codes[:], w2_raw[:, t::PACK])
+            else:
+                nc.vector.tensor_copy(codes[:], w2_raw[:, t::PACK])
+            b_res.append(product("b%d" % t, codes[:].bitcast(FP8X4), scales[:], xo_codes[:].bitcast(FP4X4), xo_sc[:]))
+
+        xt_sc = sb("xt_sc", [P, J], U8)
+        nc.vector.tensor_copy(xt_sc[:], xt_plane[:].indirect(l1[:]))
+        xt_codes = sb("xt_codes", [P, J], U32)
+        nc.vector.tensor_copy(xt_codes[:], xt_win[:].indirect(l1[:]))
+        w_dealt = sb("w_dealt", [P, PACK, P, 2], U8)
+        nc.vector.tensor_copy(w_dealt[:], w_raw[:].rearrange("p (m t b) -> p t m b", t=PACK, b=2))
+        ws_dealt = sb("ws_dealt", [P, PACK, P], U8)
+        nc.vector.tensor_copy(ws_dealt[:], w_plane[:].rearrange("p (m t) -> p t m", t=PACK))
+        a_res = []
+        for t in range(PACK):
+            a_res.append(product("a%d" % t, w_dealt[:, t, :, :].rearrange("p m b -> p (m b)").bitcast(FP4X4), ws_dealt[:, t, :], xt_codes[:].bitcast(FP8X4), xt_sc[:]))
+
+        gates = [sb("g%d" % t, [P, O], F32) for t in range(PACK)]
+        values = [sb("v%d" % t, [P, O], F32) for t in range(PACK)]
+        hid = [sb("hid%d" % h, [P, HALF, PACK], BF16) for h in range(2)]
+
+        def put_gate(t):
+            nc.scalar.activation(gate_boards[t % 2][:].indirect(l4[:]), b_res[t][:], ACT.Copy)
+
+        def put_value(t):
+            nc.scalar.activation(value_boards[t % 2][:].indirect(l3[:]), a_res[t][:], ACT.Copy)
+
+        def get_gate(t):
+            nc.scalar.activation(gates[t][:], gate_boards[t % 2][:].indirect(l6[:]), ACT.Sigmoid, scale=slope[:, t : t + 1], bias=offset[:, t : t + 1])
+
+        def get_value(t, lo, hi):
+            nc.scalar.activation(values[t][:, lo:hi], value_boards[t % 2][:].indirect(l5[:, lo // 16 : hi // 16]), ACT.Copy, scale=weight[:, t : t + 1])
+
+        def gated(t, h):
+            cols = slice(h * HALF, (h + 1) * HALF)
+            nc.vector.tensor_tensor(hid[h][:, :, t], values[t][:, cols], gates[t][:, cols], MULT)
+
+        def finish(h):
+            codes = sb("hc%d" % h, [P, HALF], U32)
+            scales = sb("hs%d" % h, [P, HALF], U8)
+            nc.vector.quantize_mx(out=codes[:].bitcast(FP8X4), scales=scales[:], in_=hid[h][:].rearrange("p o t -> p (o t)"))
+            for n in range(2):
+                rows = slice(n * P, (n + 1) * P)
+                acc = psum.tile([P, HALF], F32, name="acc_out")
+                nc.tensor.matmul_mx(out=acc[:], lhsT=wb_codes[:, rows].bitcast(FP8X4), lhsT_scale=wb_plane[:, rows], rhs=codes[:].bitcast(FP8X4), rhs_scale=scales[:], start=True, stop=True)
+                res = sb("y%d%d" % (h, n), [P, HALF], F32)
+                if n == 0:
+                    nc.scalar.copy(res[:], acc[:])
+                    nc.scalar.dma_start(out[rows, h * HALF : (h + 1) * HALF], res[:])
+                else:
+                    nc.vector.tensor_copy(res[:], acc[:])
+                    nc.sync.dma_start(out[rows, h * HALF : (h + 1) * HALF], res[:])
+
+        put_gate(0)
+        put_gate(1)
+        get_gate(0)
+        put_gate(2)
+        get_gate(1)
+        put_gate(3)
+        get_gate(2)
+        put_value(0)
+        put_value(1)
+        get_value(0, 0, O)
+        gated(0, 0)
+        gated(0, 1)
+        put_value(2)
+        get_value(1, 0, O)
+        gated(1, 0)
+        gated(1, 1)
+        get_value(2, 0, O)
+        gated(2, 0)
+        gated(2, 1)
+        put_value(3)
+        get_gate(3)
+        get_value(3, 0, HALF)
+        gated(3, 0)
+        get_value(3, HALF, O)
+        gated(3, 1)
+        finish(0)
+        finish(1)

@@ -30,16 +30,16 @@ def tile_picked_tokens_gate_two_sigmoidboard_one_plain_kernel(
         keep = ctx.enter_context(tc.tile_pool(name="keep", bufs=1))
         psum = ctx.enter_context(tc.psum_pool(name="psum", bufs=4))
 
-        def sb(name, shape, dtype):
-            return keep.tile(shape, dtype, name=name, align_bytes=64)
+        def sb(name, shape, dtype, tag=None):
+            return keep.tile(shape, dtype, name=name, tag=tag or name, align_bytes=64)
 
         def load_list(name, src):
             lst = sb(name, [P, J // 16], U16)
             nc.sync.dma_start(lst[:], src)
             return lst
 
-        def zeroed_plane(name, width):
-            plane = sb(name, [P, width], U8)
+        def zeroed_plane(name, width, tag):
+            plane = sb(name, [P, width], U8, tag)
             nc.vector.memset(plane[:].bitcast(I32), 0)
             return plane
 
@@ -52,67 +52,65 @@ def tile_picked_tokens_gate_two_sigmoidboard_one_plain_kernel(
             nc.sync.dma_start(col[:], src.rearrange("(p t) o -> p (t o)", t=PACK))
             return col
 
-        xo_plane = zeroed_plane("xo_plane", M)
-        w2_plane = zeroed_plane("w2_plane", R)
-        xt_plane = zeroed_plane("xt_plane", T)
-        w_plane = zeroed_plane("w_plane", R)
-        wb_plane = zeroed_plane("wb_plane", N)
+        xo_plane = zeroed_plane("xo_plane", M, "table_scales")
+        w2_plane = zeroed_plane("w2_plane", R, "matrix_scales")
         gate_boards = [sb("pv%d" % i, [P, C], F32) for i in range(2)]
         value_boards = [sb("pw%d" % i, [P, C], F32) for i in range(2)]
         for board in gate_boards + value_boards:
             nc.vector.memset(board[:], 0.0)
 
-        xo_win = sb("xo_win", [P, M], U16)
-        nc.scalar.dma_start(xo_win[:].bitcast(I32), xo_words[0].bitcast(I32))
-        w2_raw = sb("w2_raw", [P, R], U32)
-        nc.scalar.dma_start(w2_raw[:].bitcast(I32), w2_words[0].rearrange("p n t -> p (n t)").bitcast(I32))
         l2 = load_list("l2", offs2)
-        w2_stage = sb("w2_stage", [4, QUADS, R // 4], I32)
-        nc.sync.dma_start(w2_stage[:], w2_scales[0].bitcast(I32).rearrange("(q i) n -> i q n", i=4))
-        load_plane(xo_plane, xo_scales)
         l4 = load_list("l4", offs4)
-        l1 = load_list("l1", offs)
-        load_plane(xt_plane, xt_scales)
-        xt_win = sb("xt_win", [P, T], U32)
-        nc.sync.dma_start(xt_win[:].bitcast(I32), xt_words[0].rearrange("p n t -> p (n t)").bitcast(I32))
-        w_raw = sb("w_raw", [P, 2 * R], U8)
-        nc.sync.dma_start(w_raw[:].bitcast(I32), w_words[0].bitcast(I32))
+        load_plane(xo_plane, xo_scales)
+        xo_win = sb("xo_win", [P, M], U16, "table")
+        nc.sync.dma_start(xo_win[:].bitcast(I32), xo_words[0].bitcast(I32))
+        w2_raw = sb("w2_raw", [P, R], U32, "matrix")
+        nc.sync.dma_start(w2_raw[:].bitcast(I32), w2_words[0].rearrange("p n t -> p (n t)").bitcast(I32))
+        load_plane(w2_plane, w2_scales)
         l6 = load_list("l6", offs6)
         slope = load_rows("slope", sl)
         offset = load_rows("offset", gf)
-        load_plane(w_plane, w_scales)
+        l1 = load_list("l1", offs)
         l3 = load_list("l3", offs3)
         l5 = load_list("l5", offs5)
         weight = load_rows("weight", sa)
-        wb_codes = sb("wb_codes", [P, N], U32)
-        nc.sync.dma_start(wb_codes[:].bitcast(I32), wb_words[0].rearrange("p n t -> p (n t)").bitcast(I32))
-        load_plane(wb_plane, wb_scales)
 
-        for q in range(QUADS):
-            nc.vector.tensor_copy(w2_plane[32 * q : 32 * q + 4, :].bitcast(I32), w2_stage[0:4, q, :])
-        xo_sc = sb("xo_sc", [P, J], U8)
-        nc.vector.tensor_copy(xo_sc[:], xo_plane[:].indirect(l2[:]))
-        xo_codes = sb("xo_codes", [P, J], U16)
-        nc.vector.tensor_copy(xo_codes[:], xo_win[:].indirect(l2[:]))
-
-        def product(name, codes, scales, rhs, rhs_scale):
+        def product(name, codes, scales, rhs, rhs_scale, first=False):
             acc = psum.tile([P, J], F32, name="acc")
             nc.tensor.matmul_mx(out=acc[:], lhsT=codes, lhsT_scale=scales, rhs=rhs, rhs_scale=rhs_scale, start=True, stop=True)
             res = sb(name, [P, J], F32)
-            nc.vector.tensor_copy(res[:], acc[:])
+            if first:
+                nc.scalar.copy(res[:], acc[:])
+            else:
+                nc.vector.tensor_copy(res[:], acc[:])
             return res
 
+        xo_sc = sb("xo_sc", [P, J], U8)
+        xo_codes = sb("xo_codes", [P, J], U16)
+        w2c0 = sb("w2c0", [P, P], U32)
+        w2s0 = sb("w2s0", [P, P], U8)
+        w2c_rest = sb("w2c_rest", [P, PACK - 1, P], U32)
+        w2s_rest = sb("w2s_rest", [P, PACK - 1, P], U8)
+        w2c = [w2c0[:]] + [w2c_rest[:, t, :] for t in range(PACK - 1)]
+        w2s = [w2s0[:]] + [w2s_rest[:, t, :] for t in range(PACK - 1)]
         b_res = []
+        nc.vector.tensor_copy(xo_sc[:], xo_plane[:].indirect(l2[:]))
+        nc.vector.tensor_copy(xo_codes[:], xo_win[:].indirect(l2[:]))
+        nc.scalar.copy(w2c0[:], w2_raw[:, 0::PACK])
+        nc.scalar.copy(w2c_rest[:], w2_raw[:].rearrange("p (m t) -> p t m", t=PACK)[:, 1:PACK, :])
+        nc.vector.tensor_copy(w2s0[:], w2_plane[:, 0::PACK])
+        nc.vector.tensor_copy(w2s_rest[:], w2_plane[:].rearrange("p (m t) -> p t m", t=PACK)[:, 1:PACK, :])
         for t in range(PACK):
-            codes = sb("w2c%d" % t, [P, P], U32)
-            scales = sb("w2s%d" % t, [P, P], U8)
-            nc.vector.tensor_copy(scales[:], w2_plane[:, t::PACK])
-            if t == 0:
-                nc.scalar.copy(codes[:], w2_raw[:, t::PACK])
-            else:
-                nc.vector.tensor_copy(codes[:], w2_raw[:, t::PACK])
-            b_res.append(product("b%d" % t, codes[:].bitcast(FP8X4), scales[:], xo_codes[:].bitcast(FP4X4), xo_sc[:]))
+            b_res.append(product("b%d" % t, w2c[t].bitcast(FP8X4), w2s[t], xo_codes[:].bitcast(FP4X4), xo_sc[:], t == 0))
 
+        xt_win = sb("xt_win", [P, T], U32, "table")
+        nc.sync.dma_start(xt_win[:].bitcast(I32), xt_words[0].rearrange("p n t -> p (n t)").bitcast(I32))
+        w_raw = sb("w_raw", [P, 2 * R], U8, "matrix")
+        nc.sync.dma_start(w_raw[:].bitcast(I32), w_words[0].bitcast(I32))
+        xt_plane = zeroed_plane("xt_plane", T, "table_scales")
+        load_plane(xt_plane, xt_scales)
+        w_plane = zeroed_plane("w_plane", R, "matrix_scales")
+        load_plane(w_plane, w_scales)
         xt_sc = sb("xt_sc", [P, J], U8)
         nc.vector.tensor_copy(xt_sc[:], xt_plane[:].indirect(l1[:]))
         xt_codes = sb("xt_codes", [P, J], U32)
@@ -121,12 +119,16 @@ def tile_picked_tokens_gate_two_sigmoidboard_one_plain_kernel(
         nc.vector.tensor_copy(w_dealt[:], w_raw[:].rearrange("p (m t b) -> p t m b", t=PACK, b=2))
         ws_dealt = sb("ws_dealt", [P, PACK, P], U8)
         nc.vector.tensor_copy(ws_dealt[:], w_plane[:].rearrange("p (m t) -> p t m", t=PACK))
+        wb_codes = sb("wb_codes", [P, N], U32, "matrix")
+        nc.sync.dma_start(wb_codes[:].bitcast(I32), wb_words[0].rearrange("p n t -> p (n t)").bitcast(I32))
+        wb_plane = zeroed_plane("wb_plane", N, "matrix_scales")
+        load_plane(wb_plane, wb_scales)
         a_res = []
         for t in range(PACK):
             a_res.append(product("a%d" % t, w_dealt[:, t, :, :].rearrange("p m b -> p (m b)").bitcast(FP4X4), ws_dealt[:, t, :], xt_codes[:].bitcast(FP8X4), xt_sc[:]))
 
-        gates = [sb("g%d" % t, [P, O], F32) for t in range(PACK)]
-        values = [sb("v%d" % t, [P, O], F32) for t in range(PACK)]
+        gates = [sb("g%d" % u, [P, 2, O], F32) for u in range(2)]
+        values = [sb("v%d" % u, [P, 2, O], F32) for u in range(2)]
         hid = [sb("hid%d" % h, [P, HALF, PACK], BF16) for h in range(2)]
 
         def put_gate(t):
@@ -136,55 +138,61 @@ def tile_picked_tokens_gate_two_sigmoidboard_one_plain_kernel(
             nc.scalar.activation(value_boards[t % 2][:].indirect(l3[:]), a_res[t][:], ACT.Copy)
 
         def get_gate(t):
-            nc.scalar.activation(gates[t][:], gate_boards[t % 2][:].indirect(l6[:]), ACT.Sigmoid, scale=slope[:, t : t + 1], bias=offset[:, t : t + 1])
+            nc.scalar.activation(gates[t // 2][:, t % 2, :], gate_boards[t % 2][:].indirect(l6[:]), ACT.Sigmoid, scale=slope[:, t : t + 1], bias=offset[:, t : t + 1])
 
         def get_value(t, lo, hi):
-            nc.scalar.activation(values[t][:, lo:hi], value_boards[t % 2][:].indirect(l5[:, lo // 16 : hi // 16]), ACT.Copy, scale=weight[:, t : t + 1])
+            nc.scalar.activation(values[t // 2][:, t % 2, lo:hi], value_boards[t % 2][:].indirect(l5[:, lo // 16 : hi // 16]), ACT.Copy, scale=weight[:, t : t + 1])
 
-        def gated(t, h):
+        def gated(u, h):
             cols = slice(h * HALF, (h + 1) * HALF)
-            nc.vector.tensor_tensor(hid[h][:, :, t], values[t][:, cols], gates[t][:, cols], MULT)
+            nc.vector.tensor_tensor(hid[h][:, :, 2 * u : 2 * u + 2], values[u][:, :, cols].rearrange("p e o -> p o e"), gates[u][:, :, cols].rearrange("p e o -> p o e"), MULT)
 
         def finish(h):
             codes = sb("hc%d" % h, [P, HALF], U32)
             scales = sb("hs%d" % h, [P, HALF], U8)
             nc.vector.quantize_mx(out=codes[:].bitcast(FP8X4), scales=scales[:], in_=hid[h][:].rearrange("p o t -> p (o t)"))
-            for n in range(2):
-                rows = slice(n * P, (n + 1) * P)
-                acc = psum.tile([P, HALF], F32, name="acc_out")
-                nc.tensor.matmul_mx(out=acc[:], lhsT=wb_codes[:, rows].bitcast(FP8X4), lhsT_scale=wb_plane[:, rows], rhs=codes[:].bitcast(FP8X4), rhs_scale=scales[:], start=True, stop=True)
-                res = sb("y%d%d" % (h, n), [P, HALF], F32)
-                if n == 0:
-                    nc.scalar.copy(res[:], acc[:])
-                    nc.scalar.dma_start(out[rows, h * HALF : (h + 1) * HALF], res[:])
-                else:
-                    nc.vector.tensor_copy(res[:], acc[:])
-                    nc.sync.dma_start(out[rows, h * HALF : (h + 1) * HALF], res[:])
+            cols = slice(h * HALF, (h + 1) * HALF)
 
-        put_gate(0)
-        put_gate(1)
-        get_gate(0)
-        put_gate(2)
-        get_gate(1)
-        put_gate(3)
-        get_gate(2)
+            def multiply(acc, n):
+                rows = slice(n * P, (n + 1) * P)
+                nc.tensor.matmul_mx(out=acc, lhsT=wb_codes[:, rows].bitcast(FP8X4), lhsT_scale=wb_plane[:, rows], rhs=codes[:].bitcast(FP8X4), rhs_scale=scales[:], start=True, stop=True)
+
+            if h == 0:
+                acc = psum.tile([P, 2, HALF], F32, name="acc")
+                res = sb("y0", [P, 2, HALF], F32)
+                for n in range(2):
+                    multiply(acc[:, n, :], n)
+                nc.scalar.copy(res[:], acc[:])
+                nc.sync.dma_start(out[:, cols].rearrange("(n p) o -> p n o", p=P), res[:])
+            else:
+                for n in range(2):
+                    acc = psum.tile([P, HALF], F32, name="acc_out")
+                    res = sb("y1%d" % n, [P, HALF], F32)
+                    multiply(acc[:], n)
+                    if n == 0:
+                        nc.scalar.copy(res[:], acc[:])
+                        nc.scalar.dma_start(out[n * P : (n + 1) * P, cols], res[:])
+                    else:
+                        nc.vector.tensor_copy(res[:], acc[:])
+                        nc.sync.dma_start(out[n * P : (n + 1) * P, cols], res[:])
+
+        for u in range(2):
+            put_gate(2 * u)
+            put_gate(2 * u + 1)
+            get_gate(2 * u)
+            get_gate(2 * u + 1)
         put_value(0)
         put_value(1)
         get_value(0, 0, O)
+        get_value(1, 0, O)
         gated(0, 0)
         gated(0, 1)
         put_value(2)
-        get_value(1, 0, O)
+        put_value(3)
+        get_value(2, 0, O)
+        get_value(3, 0, HALF)
+        get_value(3, HALF, O)
         gated(1, 0)
         gated(1, 1)
-        get_value(2, 0, O)
-        gated(2, 0)
-        gated(2, 1)
-        put_value(3)
-        get_gate(3)
-        get_value(3, 0, HALF)
-        gated(3, 0)
-        get_value(3, HALF, O)
-        gated(3, 1)
         finish(0)
         finish(1)

from contextlib import ExitStack

import concourse.mybir as mybir

F32 = mybir.dt.float32
BF16 = mybir.dt.bfloat16
I32 = mybir.dt.int32
U32 = mybir.dt.uint32
U16 = mybir.dt.uint16
U8 = mybir.dt.uint8
FP8X4 = mybir.dt.float8_e4m3fn_x4
FP4X4 = mybir.dt.float4_e2m1fn_x4
ACT = mybir.ActivationFunctionType
MULT = mybir.AluOpType.mult

K, J, R, T, Z, M, C, O, N = 512, 256, 512, 1024, 512, 1024, 512, 256, 256
P = 128
PACK = 4
QUADS = 4
HALF = O // 2
FLOPS = 2 * K * R * J + 2 * Z * R * J + 2 * R * N * O


def tile_picked_tokens_gate_two_sigmoidboard_one_plain_kernel(
    tc, xt_words, xt_scales, w_words, w_scales, xo_words, xo_scales, w2_words, w2_scales,
    sl, gf, sa, wb_words, wb_scales, offs, offs2, offs3, offs4, offs5, offs6, out,
):
    nc = tc.nc
    with ExitStack() as ctx:
        keep = ctx.enter_context(tc.tile_pool(name="keep", bufs=1))
        psum = ctx.enter_context(tc.psum_pool(name="psum", bufs=4))

        def sb(name, shape, dtype, tag=None):
            return keep.tile(shape, dtype, name=name, tag=tag or name, align_bytes=64)

        def load_list(name, src):
            lst = sb(name, [P, J // 16], U16)
            nc.sync.dma_start(lst[:], src)
            return lst

        def zeroed_plane(name, width, tag):
            plane = sb(name, [P, width], U8, tag)
            nc.vector.memset(plane[:].bitcast(I32), 0)
            return plane

        def load_plane(plane, scales):
            for q in range(QUADS):
                nc.sync.dma_start(plane[32 * q : 32 * q + 4, :].bitcast(I32), scales[0, 4 * q : 4 * q + 4, :].bitcast(I32))

        def load_rows(name, src):
            col = sb(name, [P, PACK], F32)
            nc.sync.dma_start(col[:], src.rearrange("(p t) o -> p (t o)", t=PACK))
            return col

        xo_plane = zeroed_plane("xo_plane", M, "table_scales")
        w2_plane = zeroed_plane("w2_plane", R, "matrix_scales")
        gate_boards = [sb("pv%d" % i, [P, C], F32) for i in range(2)]
        value_boards = [sb("pw%d" % i, [P, C], F32) for i in range(2)]
        for board in gate_boards + value_boards:
            nc.vector.memset(board[:], 0.0)

        l2 = load_list("l2", offs2)
        l4 = load_list("l4", offs4)
        load_plane(xo_plane, xo_scales)
        xo_win = sb("xo_win", [P, M], U16, "table")
        nc.sync.dma_start(xo_win[:].bitcast(I32), xo_words[0].bitcast(I32))
        w2_raw = sb("w2_raw", [P, R], U32, "matrix")
        nc.sync.dma_start(w2_raw[:].bitcast(I32), w2_words[0].rearrange("p n t -> p (n t)").bitcast(I32))
        load_plane(w2_plane, w2_scales)
        l6 = load_list("l6", offs6)
        slope = load_rows("slope", sl)
        offset = load_rows("offset", gf)
        l1 = load_list("l1", offs)
        l3 = load_list("l3", offs3)
        l5 = load_list("l5", offs5)
        weight = load_rows("weight", sa)

        def product(name, codes, scales, rhs, rhs_scale, first=False):
            acc = psum.tile([P, J], F32, name="acc")
            nc.tensor.matmul_mx(out=acc[:], lhsT=codes, lhsT_scale=scales, rhs=rhs, rhs_scale=rhs_scale, start=True, stop=True)
            res = sb(name, [P, J], F32)
            if first:
                nc.scalar.copy(res[:], acc[:])
            else:
                nc.vector.tensor_copy(res[:], acc[:])
            return res

        xo_sc = sb("xo_sc", [P, J], U8)
        xo_codes = sb("xo_codes", [P, J], U16)
        w2c0 = sb("w2c0", [P, P], U32)
        w2s0 = sb("w2s0", [P, P], U8)
        w2c_rest = sb("w2c_rest", [P, PACK - 1, P], U32)
        w2s_rest = sb("w2s_rest", [P, PACK - 1, P], U8)
        w2c = [w2c0[:]] + [w2c_rest[:, t, :] for t in range(PACK - 1)]
        w2s = [w2s0[:]] + [w2s_rest[:, t, :] for t in range(PACK - 1)]
        b_res = []
        nc.vector.tensor_copy(xo_sc[:], xo_plane[:].indirect(l2[:]))
        nc.vector.tensor_copy(xo_codes[:], xo_win[:].indirect(l2[:]))
        nc.scalar.copy(w2c0[:], w2_raw[:, 0::PACK])
        nc.scalar.copy(w2c_rest[:], w2_raw[:].rearrange("p (m t) -> p t m", t=PACK)[:, 1:PACK, :])
        nc.vector.tensor_copy(w2s0[:], w2_plane[:, 0::PACK])
        nc.vector.tensor_copy(w2s_rest[:], w2_plane[:].rearrange("p (m t) -> p t m", t=PACK)[:, 1:PACK, :])
        for t in range(PACK):
            b_res.append(product("b%d" % t, w2c[t].bitcast(FP8X4), w2s[t], xo_codes[:].bitcast(FP4X4), xo_sc[:], t == 0))

        xt_win = sb("xt_win", [P, T], U32, "table")
        nc.sync.dma_start(xt_win[:].bitcast(I32), xt_words[0].rearrange("p n t -> p (n t)").bitcast(I32))
        w_raw = sb("w_raw", [P, 2 * R], U8, "matrix")
        nc.sync.dma_start(w_raw[:].bitcast(I32), w_words[0].bitcast(I32))
        xt_plane = zeroed_plane("xt_plane", T, "table_scales")
        load_plane(xt_plane, xt_scales)
        w_plane = zeroed_plane("w_plane", R, "matrix_scales")
        load_plane(w_plane, w_scales)
        xt_sc = sb("xt_sc", [P, J], U8)
        nc.vector.tensor_copy(xt_sc[:], xt_plane[:].indirect(l1[:]))
        xt_codes = sb("xt_codes", [P, J], U32)
        nc.vector.tensor_copy(xt_codes[:], xt_win[:].indirect(l1[:]))
        w_dealt = sb("w_dealt", [P, PACK, P, 2], U8)
        nc.vector.tensor_copy(w_dealt[:], w_raw[:].rearrange("p (m t b) -> p t m b", t=PACK, b=2))
        ws_dealt = sb("ws_dealt", [P, PACK, P], U8)
        nc.vector.tensor_copy(ws_dealt[:], w_plane[:].rearrange("p (m t) -> p t m", t=PACK))
        wb_codes = sb("wb_codes", [P, N], U32, "matrix")
        nc.sync.dma_start(wb_codes[:].bitcast(I32), wb_words[0].rearrange("p n t -> p (n t)").bitcast(I32))
        wb_plane = zeroed_plane("wb_plane", N, "matrix_scales")
        load_plane(wb_plane, wb_scales)
        a_res = []
        for t in range(PACK):
            a_res.append(product("a%d" % t, w_dealt[:, t, :, :].rearrange("p m b -> p (m b)").bitcast(FP4X4), ws_dealt[:, t, :], xt_codes[:].bitcast(FP8X4), xt_sc[:]))

        gates = [sb("g%d" % u, [P, 2, O], F32) for u in range(2)]
        values = [sb("v%d" % u, [P, 2, O], F32) for u in range(2)]
        hid = [sb("hid%d" % h, [P, HALF, PACK], BF16) for h in range(2)]

        def put_gate(t):
            nc.scalar.activation(gate_boards[t % 2][:].indirect(l4[:]), b_res[t][:], ACT.Copy)

        def put_value(t):
            nc.scalar.activation(value_boards[t % 2][:].indirect(l3[:]), a_res[t][:], ACT.Copy)

        def get_gate(t):
            nc.scalar.activation(gates[t // 2][:, t % 2, :], gate_boards[t % 2][:].indirect(l6[:]), ACT.Sigmoid, scale=slope[:, t : t + 1], bias=offset[:, t : t + 1])

        def get_value(t, lo, hi):
            nc.scalar.activation(values[t // 2][:, t % 2, lo:hi], value_boards[t % 2][:].indirect(l5[:, lo // 16 : hi // 16]), ACT.Copy, scale=weight[:, t : t + 1])

        def gated(u, h):
            cols = slice(h * HALF, (h + 1) * HALF)
            nc.vector.tensor_tensor(hid[h][:, :, 2 * u : 2 * u + 2], values[u][:, :, cols].rearrange("p e o -> p o e"), gates[u][:, :, cols].rearrange("p e o -> p o e"), MULT)

        def finish(h):
            codes = sb("hc%d" % h, [P, HALF], U32)
            scales = sb("hs%d" % h, [P, HALF], U8)
            nc.vector.quantize_mx(out=codes[:].bitcast(FP8X4), scales=scales[:], in_=hid[h][:].rearrange("p o t -> p (o t)"))
            cols = slice(h * HALF, (h + 1) * HALF)

            def multiply(acc, n):
                rows = slice(n * P, (n + 1) * P)
                nc.tensor.matmul_mx(out=acc, lhsT=wb_codes[:, rows].bitcast(FP8X4), lhsT_scale=wb_plane[:, rows], rhs=codes[:].bitcast(FP8X4), rhs_scale=scales[:], start=True, stop=True)

            if h == 0:
                acc = psum.tile([P, 2, HALF], F32, name="acc")
                res = sb("y0", [P, 2, HALF], F32)
                for n in range(2):
                    multiply(acc[:, n, :], n)
                nc.scalar.copy(res[:], acc[:])
                nc.sync.dma_start(out[:, cols].rearrange("(n p) o -> p n o", p=P), res[:])
            else:
                for n in range(2):
                    acc = psum.tile([P, HALF], F32, name="acc_out")
                    res = sb("y1%d" % n, [P, HALF], F32)
                    multiply(acc[:], n)
                    if n == 0:
                        nc.scalar.copy(res[:], acc[:])
                        nc.scalar.dma_start(out[n * P : (n + 1) * P, cols], res[:])
                    else:
                        nc.vector.tensor_copy(res[:], acc[:])
                        nc.sync.dma_start(out[n * P : (n + 1) * P, cols], res[:])

        for u in range(2):
            put_gate(2 * u)
            put_gate(2 * u + 1)
            get_gate(2 * u)
            get_gate(2 * u + 1)
        put_value(0)
        put_value(1)
        get_value(0, 0, O)
        get_value(1, 0, O)
        gated(0, 0)
        gated(0, 1)
        put_value(2)
        put_value(3)
        get_value(2, 0, O)
        get_value(3, 0, HALF)
        get_value(3, HALF, O)
        gated(1, 0)
        gated(1, 1)
        finish(0)
        finish(1)
